import numpy as np
import ml_dtypes


def mxq(x, axis, fmt="e4m3"):
    dtype, down = {"e4m3": (ml_dtypes.float8_e4m3fn, 7), "e5m2": (ml_dtypes.float8_e5m2, 14)}[fmt]
    v = np.moveaxis(np.asarray(x, np.float32).astype(ml_dtypes.bfloat16).astype(np.float64), axis, -1)
    blocks = v.reshape(v.shape[:-1] + (-1, 32))
    amax = np.abs(blocks).max(-1, keepdims=True)
    byte = np.maximum(np.where(amax > 0, np.frexp(amax)[1] - 1 + 127, 0) - down, 1)
    scale = np.exp2(byte - 127.0)
    codes = (blocks / scale).astype(np.float32).astype(dtype).astype(np.float64)
    return np.moveaxis((codes * scale).reshape(v.shape), -1, axis)


WIDE = False


def mx_kscale(k):
    if not WIDE:
        return np.ones(k)
    levels = np.array([10, -10, 5, -5, 0])
    if k % 512:
        return np.exp2(np.random.permutation(np.resize(levels, k // 32))).repeat(32)
    a = np.empty((k // 512, 16))
    for p in range(k // 512):
        a[p, :8] = np.random.permutation(np.resize(levels, 8))
        for g in range(8):
            far = levels[np.abs(levels - a[p, g]) >= 10]
            a[p, g + 8] = far[np.random.randint(len(far))]
    return np.exp2(a.ravel()).repeat(32)


def f64(x):
    return np.asarray(x).astype(np.float64)


def striped(idx):
    return np.tile(idx.reshape(-1, 16).T, (8, 1)).astype(np.uint16)


def unstriped(offs):
    return offs[:16].T.reshape(-1).astype(np.int64)


def pack_weight(w):
    k, n = w.shape
    w = f64(np.asarray(w, np.float32).astype(ml_dtypes.bfloat16)).reshape(k // 32, 32, n)
    amax = np.abs(w).max(1)
    byte = np.clip(np.where(amax > 0, np.frexp(amax)[1] - 1 + 127 - 7, 1), 1, 254)
    scaled = (w * np.exp2(127.0 - byte)[:, None, :]).reshape(k, n).astype(np.float32)
    words = np.ascontiguousarray(scaled.reshape(k // 512, 128, 4, n).transpose(0, 1, 3, 2)).astype(ml_dtypes.float8_e4m3fn).view(np.uint8)
    return words, np.ascontiguousarray(byte.astype(np.uint8).reshape(k // 512, 16, n))


def unpack_weight(words, scales):
    g, p, n, _ = words.shape
    vals = np.ascontiguousarray(words).view(ml_dtypes.float8_e4m3fn).astype(np.float64) * np.repeat(np.exp2(scales.astype(np.float64) - 127.0), 8, axis=1)[..., None]
    return vals.transpose(0, 1, 3, 2).reshape(g * 512, n)


K, T, S, N, H, U = 1024, 2048, 512, 128, 512, 1024


def setup_inputs():
    n = np.random.standard_normal
    s = mx_kscale(K)[:, None]
    u = mx_kscale(H)
    packed_xT = pack_weight(n((K, T)) * s)
    return {
        "x_words": packed_xT[0],
        "x_scales": packed_xT[1],
        "w1": (n((K, H)) / np.sqrt(K) / s).astype(np.float32),
        "unit": (np.random.uniform(0.6, 1.4, (H, 1)) * u[:, None]).astype(np.float32),
        "w2": (n((H, N)) / np.sqrt(H) / u[:, None]).astype(np.float32),
        "offs": striped(np.random.permutation(T)[:S]),
        "f1": striped(np.random.permutation(np.concatenate([np.arange(S), np.random.randint(0, S, U - S)]))),
        "f2": striped(np.random.permutation(np.concatenate([np.arange(S), np.random.randint(0, S, U - S)]))),
        "f3": striped(np.random.permutation(np.concatenate([np.arange(S), np.random.randint(0, S, U - S)]))),
        "f4": striped(np.random.permutation(np.concatenate([np.arange(S), np.random.randint(0, S, U - S)]))),
    }


def reference(x_words, x_scales, w1, unit, w2, offs, f1, f2, f3, f4):
    xq = unpack_weight(x_words, x_scales)[:, unstriped(offs)]
    y = mxq(f64(w1), 0, "e4m3").T @ xq
    y1 = y[:, unstriped(f1)]
    y3 = y[:, unstriped(f3)]
    dia = y1 + y3
    y2 = y[:, unstriped(f2)]
    y4 = y[:, unstriped(f4)]
    dib = y2 + y4
    hid = f64(unit) * (dia * dib)
    return mxq(f64(w2), 0, "e4m3").T @ mxq(hid, 0, "e4m3")

@@ -1,0 +1,156 @@
+from contextlib import ExitStack
+
+import concourse.mybir as mybir
+
+K, T, S, H, N, U = 1024, 2048, 512, 512, 128, 1024
+FLOPS = 2 * K * H * S + 2 * H * N * U
+
+F32 = mybir.dt.float32
+BF16 = mybir.dt.bfloat16
+I32 = mybir.dt.int32
+U32 = mybir.dt.uint32
+U16 = mybir.dt.uint16
+U8 = mybir.dt.uint8
+FP8X4 = mybir.dt.float8_e4m3fn_x4
+COPY = mybir.ActivationFunctionType.Copy
+ADD = mybir.AluOpType.add
+MULT = mybir.AluOpType.mult
+
+P = 128
+PACK = 4
+PASSES = K // (P * PACK)
+SPARE = 32
+CHUNKS = (512, 256, 256)
+
+
+def tile_picked_yquadfm_mul_p_kernel(tc, x_words, x_scales, w1, unit, w2, offs, f1, f2, f3, f4, out):
+    nc = tc.nc
+    with ExitStack() as ctx:
+        keep = ctx.enter_context(tc.tile_pool(name="keep", bufs=1))
+        ring = ctx.enter_context(tc.tile_pool(name="ring", bufs=4))
+        psum = ctx.enter_context(tc.psum_pool(name="psum", bufs=1))
+
+        offs_sb = keep.tile([P, S // 16], U16, name="offs_sb")
+        faces = [keep.tile([P, U // 16], U16, name=f"face{i}") for i in range(4)]
+        x_table = [keep.tile([P, T], U32, name=f"x_table{o}") for o in range(PASSES)]
+        scale_table = keep.tile([P, T], U8, name="scale_table")
+        w1_raw = [keep.tile([P, PACK, H], F32, name=f"w1_raw{o}") for o in range(PASSES)]
+        w2_raw = keep.tile([P, PACK, N], F32, name="w2_raw")
+        unit_sb = keep.tile([P, PACK], F32, name="unit_sb")
+        y_plain = [keep.tile([P, S + SPARE], F32, name=f"y_plain{t}") for t in range(PACK)]
+        y_unit = [keep.tile([P, S + SPARE], F32, name=f"y_unit{t}") for t in range(PACK)]
+
+        nc.vector.memset(scale_table[:].bitcast(I32), 0)
+        scales_i32 = x_scales.bitcast(I32)
+        for t in range(PACK):
+            nc.vector.memset(y_plain[t][:, S:], 0.0)
+            nc.vector.memset(y_unit[t][:, S:], 0.0)
+
+        def w1_rows(o):
+            return w1[o * 512 : (o + 1) * 512, :].rearrange("(p j) c -> p j c", j=PACK)
+
+        nc.sync.dma_start(out=w1_raw[0][:], in_=w1_rows(0))
+        for q in range(4):
+            nc.sync.dma_start(out=scale_table[32 * q : 32 * q + 4 * PASSES, :].bitcast(I32), in_=scales_i32[:, 4 * q : 4 * q + 4, :])
+        nc.sync.dma_start(offs_sb[:], offs)
+        nc.sync.dma_start(out=w1_raw[1][:], in_=w1_rows(1))
+        for o in range(PASSES):
+            nc.sync.dma_start(out=x_table[o][:].bitcast(I32), in_=x_words[o].rearrange("p c r -> p (c r)").bitcast(I32))
+        nc.sync.dma_start(faces[1][:], f2)
+        nc.sync.dma_start(faces[3][:], f4)
+        nc.sync.dma_start(out=unit_sb[:], in_=unit.rearrange("(p t) o -> p (t o)", t=PACK))
+        nc.sync.dma_start(faces[0][:], f1)
+        nc.sync.dma_start(faces[2][:], f3)
+        nc.sync.dma_start(out=w2_raw[:], in_=w2.rearrange("(p j) m -> p j m", j=PACK))
+
+        w1_codes, w1_scales = [], []
+        for o in range(PASSES):
+            grouped = keep.tile([P, PACK, P, PACK], BF16, name=f"w1_grouped{o}", align_bytes=64)
+            src = w1_raw[o][:].rearrange("p j (m t) -> p m j t", t=PACK)
+            dst = grouped[:].rearrange("p t m j -> p m j t")
+            if o == 0:
+                nc.scalar.activation(dst, src, COPY)
+            else:
+                nc.vector.tensor_copy(dst, src)
+            codes = keep.tile([P, H], U32, name=f"w1_codes{o}", align_bytes=64)
+            scales = keep.tile([P, H], U8, name=f"w1_scales{o}", align_bytes=64)
+            nc.vector.quantize_mx(out=codes[:].bitcast(FP8X4), scales=scales[:], in_=grouped[:].rearrange("p t m j -> p (t m j)"))
+            w1_codes.append(codes)
+            w1_scales.append(scales)
+
+        x_scale = keep.tile([P, S], U8, name="x_scale", align_bytes=64)
+        nc.vector.tensor_copy(x_scale[:], scale_table[:].indirect(offs_sb[:]))
+        x_codes = []
+        for o in range(PASSES):
+            codes = keep.tile([P, S], U32, name=f"x_codes{o}", align_bytes=64)
+            nc.vector.tensor_copy(codes[:], x_table[o][:].indirect(offs_sb[:]))
+            x_codes.append(codes)
+
+        y_banks = [psum.tile([P, S], F32, name=f"y_bank{t}") for t in range(PACK)]
+        for o in range(PASSES):
+            for t in range(PACK):
+                cols = slice(t * P, (t + 1) * P)
+                nc.tensor.matmul_mx(
+                    out=y_banks[t][:],
+                    lhsT=w1_codes[o][:, cols].bitcast(FP8X4),
+                    lhsT_scale=w1_scales[o][:, cols],
+                    rhs=x_codes[o][:].bitcast(FP8X4),
+                    rhs_scale=x_scale[4 * o : P, :],
+                    start=(o == 0),
+                    stop=(o == PASSES - 1),
+                )
+
+        w2_grouped = keep.tile([P, N, PACK], BF16, name="w2_grouped", align_bytes=64)
+        nc.vector.tensor_copy(
+            w2_grouped[:].rearrange("p (c i) j -> p c j i", i=4), w2_raw[:].rearrange("p j (c i) -> p c j i", i=4)
+        )
+        w2_codes = keep.tile([P, N], U32, name="w2_codes", align_bytes=64)
+        w2_scales = keep.tile([P, N], U8, name="w2_scales", align_bytes=64)
+        nc.vector.quantize_mx(out=w2_codes[:].bitcast(FP8X4), scales=w2_scales[:], in_=w2_grouped[:].rearrange("p m j -> p (m j)"))
+
+        def windows(t):
+            if t in (1, 2):
+                nc.vector.tensor_copy(y_plain[t][:, :S], y_banks[t][:])
+            else:
+                nc.scalar.activation(y_plain[t][:, :S], y_banks[t][:], COPY)
+            if t < 2:
+                nc.vector.tensor_scalar(y_unit[t][:, :S], y_plain[t][:, :S], unit_sb[:, t : t + 1], None, MULT)
+            else:
+                nc.scalar.activation(y_unit[t][:, :S], y_banks[t][:], COPY, scale=unit_sb[:, t : t + 1])
+
+        start = 0
+        for c, n in enumerate(CHUNKS):
+            cols = slice(start // 16, (start + n) // 16)
+            dia = keep.tile([P, PACK, n], F32, name=f"dia{c}")
+            dib = keep.tile([P, PACK, n], F32, name=f"dib{c}")
+            for t in range(PACK):
+                if c == 0:
+                    windows(t)
+                for total, window, first, second in ((dib, y_plain[t], faces[1], faces[3]), (dia, y_unit[t], faces[0], faces[2])):
+                    corner = ring.tile([P, n], F32, name="corner")
+                    nc.scalar.activation(corner[:], window[:].indirect(first[:, cols]), COPY)
+                    nc.vector.tensor_tensor(total[:, t, :], window[:].indirect(second[:, cols]), corner[:], ADD)
+            hid = keep.tile([P, n, PACK], BF16, name=f"hid{c}", align_bytes=64)
+            nc.vector.tensor_tensor(
+                hid[:].rearrange("p (c i) t -> p c t i", i=4),
+                dia[:].rearrange("p t (c i) -> p c t i", i=4),
+                dib[:].rearrange("p t (c i) -> p c t i", i=4),
+                MULT,
+            )
+            hid_codes = keep.tile([P, n], U32, name=f"hid_codes{c}", align_bytes=64)
+            hid_scales = keep.tile([P, n], U8, name=f"hid_scales{c}", align_bytes=64)
+            nc.vector.quantize_mx(out=hid_codes[:].bitcast(FP8X4), scales=hid_scales[:], in_=hid[:].rearrange("p r t -> p (r t)"))
+            acc = psum.tile([P, n], F32, name=f"acc{c}")
+            nc.tensor.matmul_mx(
+                out=acc[:],
+                lhsT=w2_codes[:].bitcast(FP8X4),
+                lhsT_scale=w2_scales[:],
+                rhs=hid_codes[:].bitcast(FP8X4),
+                rhs_scale=hid_scales[:],
+                start=True,
+                stop=True,
+            )
+            result = keep.tile([P, n], F32, name=f"result{c}")
+            nc.scalar.activation(result[:], acc[:], COPY)
+            nc.sync.dma_start(out=out[:, start : start + n], in_=result[:])
+            start = start + n

@@ -20,14 +20,15 @@ P = 128
 PACK = 4
 PASSES = K // (P * PACK)
 SPARE = 32
-CHUNKS = (512, 256, 256)
+CHUNKS = (512, 384, 128)
+W1_SPLIT = 88
 
 
 def tile_picked_yquadfm_mul_p_kernel(tc, x_words, x_scales, w1, unit, w2, offs, f1, f2, f3, f4, out):
     nc = tc.nc
     with ExitStack() as ctx:
         keep = ctx.enter_context(tc.tile_pool(name="keep", bufs=1))
-        ring = ctx.enter_context(tc.tile_pool(name="ring", bufs=4))
+        ring = ctx.enter_context(tc.tile_pool(name="ring", bufs=8))
         psum = ctx.enter_context(tc.psum_pool(name="psum", bufs=1))
 
         offs_sb = keep.tile([P, S // 16], U16, name="offs_sb")
@@ -49,19 +50,26 @@ def tile_picked_yquadfm_mul_p_kernel(tc, x_words, x_scales, w1, unit, w2, offs, 
         def w1_rows(o):
             return w1[o * 512 : (o + 1) * 512, :].rearrange("(p j) c -> p j c", j=PACK)
 
-        nc.sync.dma_start(out=w1_raw[0][:], in_=w1_rows(0))
+        def x_rows(o):
+            return x_words[o].rearrange("p c r -> p (c r)").bitcast(I32)
+
+        nc.sync.dma_start(out=x_table[0][:].bitcast(I32), in_=x_rows(0))
         for q in range(4):
             nc.sync.dma_start(out=scale_table[32 * q : 32 * q + 4 * PASSES, :].bitcast(I32), in_=scales_i32[:, 4 * q : 4 * q + 4, :])
         nc.sync.dma_start(offs_sb[:], offs)
-        nc.sync.dma_start(out=w1_raw[1][:], in_=w1_rows(1))
         for o in range(PASSES):
-            nc.sync.dma_start(out=x_table[o][:].bitcast(I32), in_=x_words[o].rearrange("p c r -> p (c r)").bitcast(I32))
-        nc.sync.dma_start(faces[1][:], f2)
-        nc.sync.dma_start(faces[3][:], f4)
+            nc.sync.dma_start(out=w1_raw[o][:], in_=w1_rows(o))
+        nc.sync.dma_start(out=x_table[1][:].bitcast(I32), in_=x_rows(1))
         nc.sync.dma_start(out=unit_sb[:], in_=unit.rearrange("(p t) o -> p (t o)", t=PACK))
-        nc.sync.dma_start(faces[0][:], f1)
-        nc.sync.dma_start(faces[2][:], f3)
         nc.sync.dma_start(out=w2_raw[:], in_=w2.rearrange("(p j) m -> p j m", j=PACK))
+        for i, face in ((1, f2), (3, f4), (0, f1), (2, f3)):
+            nc.sync.dma_start(faces[i][:], face)
+
+        x_scale = keep.tile([P, S], U8, name="x_scale", align_bytes=64)
+        nc.vector.tensor_copy(x_scale[:], scale_table[:].indirect(offs_sb[:]))
+        x_codes = [keep.tile([P, S], U32, name=f"x_codes{o}", align_bytes=64) for o in range(PASSES)]
+        halves = (slice(0, S // 2), slice(S // 2, S))
+        nc.vector.tensor_copy(x_codes[0][:], x_table[0][:].indirect(offs_sb[:]))
 
         w1_codes, w1_scales = [], []
         for o in range(PASSES):
@@ -69,67 +77,71 @@ def tile_picked_yquadfm_mul_p_kernel(tc, x_words, x_scales, w1, unit, w2, offs, 
             src = w1_raw[o][:].rearrange("p j (m t) -> p m j t", t=PACK)
             dst = grouped[:].rearrange("p t m j -> p m j t")
             if o == 0:
-                nc.scalar.activation(dst, src, COPY)
-            else:
                 nc.vector.tensor_copy(dst, src)
+            else:
+                nc.vector.tensor_copy(dst[:, :W1_SPLIT], src[:, :W1_SPLIT])
+                nc.scalar.activation(dst[:, W1_SPLIT:], src[:, W1_SPLIT:], COPY)
             codes = keep.tile([P, H], U32, name=f"w1_codes{o}", align_bytes=64)
             scales = keep.tile([P, H], U8, name=f"w1_scales{o}", align_bytes=64)
             nc.vector.quantize_mx(out=codes[:].bitcast(FP8X4), scales=scales[:], in_=grouped[:].rearrange("p t m j -> p (t m j)"))
             w1_codes.append(codes)
             w1_scales.append(scales)
 
-        x_scale = keep.tile([P, S], U8, name="x_scale", align_bytes=64)
-        nc.vector.tensor_copy(x_scale[:], scale_table[:].indirect(offs_sb[:]))
-        x_codes = []
-        for o in range(PASSES):
-            codes = keep.tile([P, S], U32, name=f"x_codes{o}", align_bytes=64)
-            nc.vector.tensor_copy(codes[:], x_table[o][:].indirect(offs_sb[:]))
-            x_codes.append(codes)
+        for half in halves:
+            nc.vector.tensor_copy(x_codes[1][:, half], x_table[1][:].indirect(offs_sb[:, half.start // 16 : half.stop // 16]))
 
-        y_banks = [psum.tile([P, S], F32, name=f"y_bank{t}") for t in range(PACK)]
+        pieces = [(t, half) for half in halves for t in range(2)] + [(t, slice(0, S)) for t in range(2, PACK)]
+        y_banks = [psum.tile([P, span.stop - span.start], F32, name=f"bank{i}") for i, (t, span) in enumerate(pieces)]
         for o in range(PASSES):
-            for t in range(PACK):
+            for bank, (t, span) in zip(y_banks, pieces):
                 cols = slice(t * P, (t + 1) * P)
                 nc.tensor.matmul_mx(
-                    out=y_banks[t][:],
+                    out=bank[:],
                     lhsT=w1_codes[o][:, cols].bitcast(FP8X4),
                     lhsT_scale=w1_scales[o][:, cols],
-                    rhs=x_codes[o][:].bitcast(FP8X4),
-                    rhs_scale=x_scale[4 * o : P, :],
+                    rhs=x_codes[o][:, span].bitcast(FP8X4),
+                    rhs_scale=x_scale[4 * o : P, span],
                     start=(o == 0),
                     stop=(o == PASSES - 1),
                 )
 
         w2_grouped = keep.tile([P, N, PACK], BF16, name="w2_grouped", align_bytes=64)
-        nc.vector.tensor_copy(
-            w2_grouped[:].rearrange("p (c i) j -> p c j i", i=4), w2_raw[:].rearrange("p j (c i) -> p c j i", i=4)
+        nc.scalar.activation(
+            w2_grouped[:].rearrange("p (c i) j -> p c j i", i=4), w2_raw[:].rearrange("p j (c i) -> p c j i", i=4), COPY
         )
         w2_codes = keep.tile([P, N], U32, name="w2_codes", align_bytes=64)
         w2_scales = keep.tile([P, N], U8, name="w2_scales", align_bytes=64)
         nc.vector.quantize_mx(out=w2_codes[:].bitcast(FP8X4), scales=w2_scales[:], in_=w2_grouped[:].rearrange("p m j -> p (m j)"))
 
-        def windows(t):
-            if t in (1, 2):
-                nc.vector.tensor_copy(y_plain[t][:, :S], y_banks[t][:])
+        for bank, (t, span) in zip(y_banks, pieces):
+            if t == 0:
+                nc.scalar.activation(y_plain[t][:, span], bank[:], COPY)
             else:
-                nc.scalar.activation(y_plain[t][:, :S], y_banks[t][:], COPY)
-            if t < 2:
-                nc.vector.tensor_scalar(y_unit[t][:, :S], y_plain[t][:, :S], unit_sb[:, t : t + 1], None, MULT)
-            else:
-                nc.scalar.activation(y_unit[t][:, :S], y_banks[t][:], COPY, scale=unit_sb[:, t : t + 1])
+                nc.vector.tensor_copy(y_plain[t][:, span], bank[:])
+        for t in range(PACK):
+            nc.vector.tensor_scalar(y_unit[t][:, :S], y_plain[t][:, :S], unit_sb[:, t : t + 1], None, MULT)
 
         start = 0
         for c, n in enumerate(CHUNKS):
             cols = slice(start // 16, (start + n) // 16)
             dia = keep.tile([P, PACK, n], F32, name=f"dia{c}")
             dib = keep.tile([P, PACK, n], F32, name=f"dib{c}")
-            for t in range(PACK):
-                if c == 0:
-                    windows(t)
-                for total, window, first, second in ((dib, y_plain[t], faces[1], faces[3]), (dia, y_unit[t], faces[0], faces[2])):
-                    corner = ring.tile([P, n], F32, name="corner")
-                    nc.scalar.activation(corner[:], window[:].indirect(first[:, cols]), COPY)
-                    nc.vector.tensor_tensor(total[:, t, :], window[:].indirect(second[:, cols]), corner[:], ADD)
+            sums = ((dib, y_plain, faces[1], faces[3]), (dia, y_unit, faces[0], faces[2]))
+            if c < len(CHUNKS) - 1:
+                for t in range(PACK):
+                    for total, windows, first, second in sums:
+                        corner = ring.tile([P, n], F32, name="corner")
+                        nc.scalar.activation(corner[:], windows[t][:].indirect(first[:, cols]), COPY)
+                        nc.vector.tensor_tensor(total[:, t, :], windows[t][:].indirect(second[:, cols]), corner[:], ADD)
+            else:
+                for total, windows, first, second in sums:
+                    pair = [ring.tile([P, PACK, n], F32, name="corner") for i in range(2)]
+                    for t in range(PACK):
+                        for corner, face in zip(pair, (first, second)):
+                            nc.scalar.activation(corner[:, t, :], windows[t][:].indirect(face[:, cols]), COPY)
+                    parts = (slice(0, PACK),) if total is dib else (slice(0, PACK - 1), slice(PACK - 1, PACK))
+                    for part in parts:
+                        nc.vector.tensor_tensor(total[:, part, :], pair[0][:, part, :], pair[1][:, part, :], ADD)
             hid = keep.tile([P, n, PACK], BF16, name=f"hid{c}", align_bytes=64)
             nc.vector.tensor_tensor(
                 hid[:].rearrange("p (c i) t -> p c t i", i=4),
@@ -140,16 +152,21 @@ def tile_picked_yquadfm_mul_p_kernel(tc, x_words, x_scales, w1, unit, w2, offs, 
             hid_codes = keep.tile([P, n], U32, name=f"hid_codes{c}", align_bytes=64)
             hid_scales = keep.tile([P, n], U8, name=f"hid_scales{c}", align_bytes=64)
             nc.vector.quantize_mx(out=hid_codes[:].bitcast(FP8X4), scales=hid_scales[:], in_=hid[:].rearrange("p r t -> p (r t)"))
-            acc = psum.tile([P, n], F32, name=f"acc{c}")
-            nc.tensor.matmul_mx(
-                out=acc[:],
-                lhsT=w2_codes[:].bitcast(FP8X4),
-                lhsT_scale=w2_scales[:],
-                rhs=hid_codes[:].bitcast(FP8X4),
-                rhs_scale=hid_scales[:],
-                start=True,
-                stop=True,
-            )
+            acc = psum.tile([P, n], F32, name=f"bank{(len(pieces) + c) % 8}")
+            done = 0
+            for width in (512, 256, 128):
+                if n - done >= width:
+                    span = slice(done, done + width)
+                    nc.tensor.matmul_mx(
+                        out=acc[:, span],
+                        lhsT=w2_codes[:].bitcast(FP8X4),
+                        lhsT_scale=w2_scales[:],
+                        rhs=hid_codes[:, span].bitcast(FP8X4),
+                        rhs_scale=hid_scales[:, span],
+                        start=True,
+                        stop=True,
+                    )
+                    done = done + width
             result = keep.tile([P, n], F32, name=f"result{c}")
             nc.scalar.activation(result[:], acc[:], COPY)
             nc.sync.dma_start(out=out[:, start : start + n], in_=result[:])

@@ -18,22 +18,30 @@ MULT = mybir.AluOpType.mult
 
 P = 128
 PACK = 4
-PASSES = K // (P * PACK)
+K_PASS = P * PACK
+PASSES = K // K_PASS
+QUADRANT = 32
+SCALE_ROWS = 4
+GROUP = 16
+LINE = 4
+BANKS = 8
 SPARE = 32
 CHUNKS = (512, 384, 128)
-W1_SPLIT = 88
+W1_ON_VECTOR = 76
+HALVED_TILES = 3
+CORNER_BUFFERS = 8
 
 
 def tile_picked_yquadfm_mul_p_kernel(tc, x_words, x_scales, w1, unit, w2, offs, f1, f2, f3, f4, out):
     nc = tc.nc
     with ExitStack() as ctx:
         keep = ctx.enter_context(tc.tile_pool(name="keep", bufs=1))
-        ring = ctx.enter_context(tc.tile_pool(name="ring", bufs=8))
+        ring = ctx.enter_context(tc.tile_pool(name="ring", bufs=CORNER_BUFFERS))
         psum = ctx.enter_context(tc.psum_pool(name="psum", bufs=1))
 
-        offs_sb = keep.tile([P, S // 16], U16, name="offs_sb")
-        faces = [keep.tile([P, U // 16], U16, name=f"face{i}") for i in range(4)]
-        x_table = [keep.tile([P, T], U32, name=f"x_table{o}") for o in range(PASSES)]
+        picks = keep.tile([P, S // GROUP], U16, name="picks")
+        list1, list2, list3, list4 = [keep.tile([P, U // GROUP], U16, name=f"list{i}") for i in range(1, 5)]
+        word_tables = [keep.tile([P, T], U32, name=f"word_table{o}") for o in range(PASSES)]
         scale_table = keep.tile([P, T], U8, name="scale_table")
         w1_raw = [keep.tile([P, PACK, H], F32, name=f"w1_raw{o}") for o in range(PASSES)]
         w2_raw = keep.tile([P, PACK, N], F32, name="w2_raw")
@@ -42,76 +50,83 @@ def tile_picked_yquadfm_mul_p_kernel(tc, x_words, x_scales, w1, unit, w2, offs, 
         y_unit = [keep.tile([P, S + SPARE], F32, name=f"y_unit{t}") for t in range(PACK)]
 
         nc.vector.memset(scale_table[:].bitcast(I32), 0)
-        scales_i32 = x_scales.bitcast(I32)
-        for t in range(PACK):
-            nc.vector.memset(y_plain[t][:, S:], 0.0)
-            nc.vector.memset(y_unit[t][:, S:], 0.0)
+        for window in y_plain + y_unit:
+            nc.vector.memset(window[:, S:], 0.0)
 
-        def w1_rows(o):
-            return w1[o * 512 : (o + 1) * 512, :].rearrange("(p j) c -> p j c", j=PACK)
+        def load_w1(o):
+            rows = w1[o * K_PASS : (o + 1) * K_PASS, :]
+            nc.sync.dma_start(out=w1_raw[o][:], in_=rows.rearrange("(p j) c -> p j c", j=PACK))
 
-        def x_rows(o):
-            return x_words[o].rearrange("p c r -> p (c r)").bitcast(I32)
+        def load_words(o):
+            words = x_words[o].rearrange("p c r -> p (c r)")
+            nc.sync.dma_start(out=word_tables[o][:].bitcast(I32), in_=words.bitcast(I32))
 
-        nc.sync.dma_start(out=x_table[0][:].bitcast(I32), in_=x_rows(0))
-        for q in range(4):
-            nc.sync.dma_start(out=scale_table[32 * q : 32 * q + 4 * PASSES, :].bitcast(I32), in_=scales_i32[:, 4 * q : 4 * q + 4, :])
-        nc.sync.dma_start(offs_sb[:], offs)
-        for o in range(PASSES):
-            nc.sync.dma_start(out=w1_raw[o][:], in_=w1_rows(o))
-        nc.sync.dma_start(out=x_table[1][:].bitcast(I32), in_=x_rows(1))
+        load_w1(0)
+        for q in range(P // QUADRANT):
+            nc.sync.dma_start(
+                out=scale_table[QUADRANT * q : QUADRANT * q + SCALE_ROWS * PASSES, :].bitcast(I32),
+                in_=x_scales.bitcast(I32)[:, SCALE_ROWS * q : SCALE_ROWS * (q + 1), :],
+            )
+        nc.sync.dma_start(picks[:], offs)
+        load_words(0)
+        load_w1(1)
+        load_words(1)
         nc.sync.dma_start(out=unit_sb[:], in_=unit.rearrange("(p t) o -> p (t o)", t=PACK))
         nc.sync.dma_start(out=w2_raw[:], in_=w2.rearrange("(p j) m -> p j m", j=PACK))
-        for i, face in ((1, f2), (3, f4), (0, f1), (2, f3)):
-            nc.sync.dma_start(faces[i][:], face)
+        for tile, face_list in ((list2, f2), (list4, f4), (list1, f1), (list3, f3)):
+            nc.sync.dma_start(tile[:], face_list)
 
-        x_scale = keep.tile([P, S], U8, name="x_scale", align_bytes=64)
-        nc.vector.tensor_copy(x_scale[:], scale_table[:].indirect(offs_sb[:]))
-        x_codes = [keep.tile([P, S], U32, name=f"x_codes{o}", align_bytes=64) for o in range(PASSES)]
-        halves = (slice(0, S // 2), slice(S // 2, S))
-        nc.vector.tensor_copy(x_codes[0][:], x_table[0][:].indirect(offs_sb[:]))
+        def quantise(grouped, width, name):
+            codes = keep.tile([P, width], U32, name=f"{name}_codes", align_bytes=64)
+            scales = keep.tile([P, width], U8, name=f"{name}_scales", align_bytes=64)
+            nc.vector.quantize_mx(out=codes[:].bitcast(FP8X4), scales=scales[:], in_=grouped)
+            return codes, scales
 
-        w1_codes, w1_scales = [], []
-        for o in range(PASSES):
+        def quantise_w1(o):
             grouped = keep.tile([P, PACK, P, PACK], BF16, name=f"w1_grouped{o}", align_bytes=64)
-            src = w1_raw[o][:].rearrange("p j (m t) -> p m j t", t=PACK)
-            dst = grouped[:].rearrange("p t m j -> p m j t")
-            if o == 0:
-                nc.vector.tensor_copy(dst, src)
-            else:
-                nc.vector.tensor_copy(dst[:, :W1_SPLIT], src[:, :W1_SPLIT])
-                nc.scalar.activation(dst[:, W1_SPLIT:], src[:, W1_SPLIT:], COPY)
-            codes = keep.tile([P, H], U32, name=f"w1_codes{o}", align_bytes=64)
-            scales = keep.tile([P, H], U8, name=f"w1_scales{o}", align_bytes=64)
-            nc.vector.quantize_mx(out=codes[:].bitcast(FP8X4), scales=scales[:], in_=grouped[:].rearrange("p t m j -> p (t m j)"))
-            w1_codes.append(codes)
-            w1_scales.append(scales)
+            source = w1_raw[o][:].rearrange("p j (m t) -> p m j t", t=PACK)
+            target = grouped[:].rearrange("p t m j -> p m j t")
+            nc.vector.tensor_copy(target[:, :W1_ON_VECTOR], source[:, :W1_ON_VECTOR])
+            nc.scalar.activation(target[:, W1_ON_VECTOR:], source[:, W1_ON_VECTOR:], COPY)
+            return quantise(grouped[:].rearrange("p t m j -> p (t m j)"), H, f"w1_{o}")
 
+        def entries(index_list, span):
+            return index_list[:, span.start // GROUP : span.stop // GROUP]
+
+        whole = slice(0, S)
+        halves = (slice(0, S // 2), slice(S // 2, S))
+        x_scale = keep.tile([P, S], U8, name="x_scale", align_bytes=64)
+        x_codes = [keep.tile([P, S], U32, name=f"x_codes{o}", align_bytes=64) for o in range(PASSES)]
+        w1_mx = [quantise_w1(0)]
+        nc.vector.tensor_copy(x_scale[:], scale_table[:].indirect(picks[:]))
+        nc.vector.tensor_copy(x_codes[0][:], word_tables[0][:].indirect(picks[:]))
+        w1_mx.append(quantise_w1(1))
         for half in halves:
-            nc.vector.tensor_copy(x_codes[1][:, half], x_table[1][:].indirect(offs_sb[:, half.start // 16 : half.stop // 16]))
+            nc.vector.tensor_copy(x_codes[1][:, half], word_tables[1][:].indirect(entries(picks, half)))
 
-        pieces = [(t, half) for half in halves for t in range(2)] + [(t, slice(0, S)) for t in range(2, PACK)]
+        pieces = [(t, half) for half in halves for t in range(HALVED_TILES)]
+        pieces = pieces + [(t, whole) for t in range(HALVED_TILES, PACK)]
         y_banks = [psum.tile([P, span.stop - span.start], F32, name=f"bank{i}") for i, (t, span) in enumerate(pieces)]
-        for o in range(PASSES):
+        for o, (w1_codes, w1_scales) in enumerate(w1_mx):
             for bank, (t, span) in zip(y_banks, pieces):
-                cols = slice(t * P, (t + 1) * P)
+                rows = slice(t * P, (t + 1) * P)
                 nc.tensor.matmul_mx(
                     out=bank[:],
-                    lhsT=w1_codes[o][:, cols].bitcast(FP8X4),
-                    lhsT_scale=w1_scales[o][:, cols],
+                    lhsT=w1_codes[:, rows].bitcast(FP8X4),
+                    lhsT_scale=w1_scales[:, rows],
                     rhs=x_codes[o][:, span].bitcast(FP8X4),
-                    rhs_scale=x_scale[4 * o : P, span],
+                    rhs_scale=x_scale[SCALE_ROWS * o : P, span],
                     start=(o == 0),
                     stop=(o == PASSES - 1),
                 )
 
         w2_grouped = keep.tile([P, N, PACK], BF16, name="w2_grouped", align_bytes=64)
         nc.scalar.activation(
-            w2_grouped[:].rearrange("p (c i) j -> p c j i", i=4), w2_raw[:].rearrange("p j (c i) -> p c j i", i=4), COPY
+            w2_grouped[:].rearrange("p (c i) j -> p c j i", i=LINE),
+            w2_raw[:].rearrange("p j (c i) -> p c j i", i=LINE),
+            COPY,
         )
-        w2_codes = keep.tile([P, N], U32, name="w2_codes", align_bytes=64)
-        w2_scales = keep.tile([P, N], U8, name="w2_scales", align_bytes=64)
-        nc.vector.quantize_mx(out=w2_codes[:].bitcast(FP8X4), scales=w2_scales[:], in_=w2_grouped[:].rearrange("p m j -> p (m j)"))
+        w2_codes, w2_scales = quantise(w2_grouped[:].rearrange("p m j -> p (m j)"), N, "w2")
 
         for bank, (t, span) in zip(y_banks, pieces):
             if t == 0:
@@ -121,38 +136,42 @@ def tile_picked_yquadfm_mul_p_kernel(tc, x_words, x_scales, w1, unit, w2, offs, 
         for t in range(PACK):
             nc.vector.tensor_scalar(y_unit[t][:, :S], y_plain[t][:, :S], unit_sb[:, t : t + 1], None, MULT)
 
-        start = 0
-        for c, n in enumerate(CHUNKS):
-            cols = slice(start // 16, (start + n) // 16)
-            dia = keep.tile([P, PACK, n], F32, name=f"dia{c}")
-            dib = keep.tile([P, PACK, n], F32, name=f"dib{c}")
-            sums = ((dib, y_plain, faces[1], faces[3]), (dia, y_unit, faces[0], faces[2]))
-            if c < len(CHUNKS) - 1:
-                for t in range(PACK):
-                    for total, windows, first, second in sums:
-                        corner = ring.tile([P, n], F32, name="corner")
-                        nc.scalar.activation(corner[:], windows[t][:].indirect(first[:, cols]), COPY)
-                        nc.vector.tensor_tensor(total[:, t, :], windows[t][:].indirect(second[:, cols]), corner[:], ADD)
-            else:
-                for total, windows, first, second in sums:
-                    pair = [ring.tile([P, PACK, n], F32, name="corner") for i in range(2)]
-                    for t in range(PACK):
-                        for corner, face in zip(pair, (first, second)):
-                            nc.scalar.activation(corner[:, t, :], windows[t][:].indirect(face[:, cols]), COPY)
-                    parts = (slice(0, PACK),) if total is dib else (slice(0, PACK - 1), slice(PACK - 1, PACK))
-                    for part in parts:
-                        nc.vector.tensor_tensor(total[:, part, :], pair[0][:, part, :], pair[1][:, part, :], ADD)
-            hid = keep.tile([P, n, PACK], BF16, name=f"hid{c}", align_bytes=64)
+        starts = [sum(CHUNKS[:c]) for c in range(len(CHUNKS))]
+        faces = [slice(start, start + n) for start, n in zip(starts, CHUNKS)]
+        dia = [keep.tile([P, PACK, n], F32, name=f"dia{c}") for c, n in enumerate(CHUNKS)]
+        dib = [keep.tile([P, PACK, n], F32, name=f"dib{c}") for c, n in enumerate(CHUNKS)]
+        hid = [keep.tile([P, n, PACK], BF16, name=f"hid{c}", align_bytes=64) for c, n in enumerate(CHUNKS)]
+        diagonals = ((dib, y_plain, list2, list4), (dia, y_unit, list1, list3))
+
+        def gather_on_scalar(target, window, index_list, c):
+            nc.scalar.activation(target, window[:].indirect(entries(index_list, faces[c])), COPY)
+
+        def shared_sum(c, t, diagonal):
+            sums, windows, first, second = diagonal
+            corner = ring.tile([P, CHUNKS[c]], F32, name="corner")
+            gather_on_scalar(corner[:], windows[t], first, c)
+            nc.vector.tensor_tensor(sums[c][:, t, :], windows[t][:].indirect(entries(second, faces[c])), corner[:], ADD)
+
+        def scalar_sums(c, tiles, diagonal):
+            sums, windows, first, second = diagonal
+            pair = [ring.tile([P, tiles, CHUNKS[c]], F32, name="corner") for index_list in (first, second)]
+            for t in range(tiles):
+                for corner, index_list in zip(pair, (first, second)):
+                    gather_on_scalar(corner[:, t, :], windows[t], index_list, c)
+            nc.vector.tensor_tensor(sums[c][:, :tiles, :], pair[0][:], pair[1][:], ADD)
+
+        def multiply(c):
             nc.vector.tensor_tensor(
-                hid[:].rearrange("p (c i) t -> p c t i", i=4),
-                dia[:].rearrange("p t (c i) -> p c t i", i=4),
-                dib[:].rearrange("p t (c i) -> p c t i", i=4),
+                hid[c][:].rearrange("p (g i) t -> p g t i", i=LINE),
+                dia[c][:].rearrange("p t (g i) -> p g t i", i=LINE),
+                dib[c][:].rearrange("p t (g i) -> p g t i", i=LINE),
                 MULT,
             )
-            hid_codes = keep.tile([P, n], U32, name=f"hid_codes{c}", align_bytes=64)
-            hid_scales = keep.tile([P, n], U8, name=f"hid_scales{c}", align_bytes=64)
-            nc.vector.quantize_mx(out=hid_codes[:].bitcast(FP8X4), scales=hid_scales[:], in_=hid[:].rearrange("p r t -> p (r t)"))
-            acc = psum.tile([P, n], F32, name=f"bank{(len(pieces) + c) % 8}")
+
+        def finish(c):
+            n = CHUNKS[c]
+            hid_codes, hid_scales = quantise(hid[c][:].rearrange("p r t -> p (r t)"), n, f"hid{c}")
+            acc = psum.tile([P, n], F32, name=f"bank{(len(pieces) + c) % BANKS}")
             done = 0
             for width in (512, 256, 128):
                 if n - done >= width:
@@ -169,5 +188,21 @@ def tile_picked_yquadfm_mul_p_kernel(tc, x_words, x_scales, w1, unit, w2, offs, 
                     done = done + width
             result = keep.tile([P, n], F32, name=f"result{c}")
             nc.scalar.activation(result[:], acc[:], COPY)
-            nc.sync.dma_start(out=out[:, start : start + n], in_=result[:])
-            start = start + n
+            nc.sync.dma_start(out=out[:, faces[c]], in_=result[:])
+
+        steps = [(t, diagonal) for t in range(PACK) for diagonal in diagonals]
+        for t, diagonal in steps:
+            shared_sum(0, t, diagonal)
+        shared_sum(1, *steps[0])
+        multiply(0)
+        shared_sum(1, *steps[1])
+        finish(0)
+        for t, diagonal in steps[2:]:
+            shared_sum(1, t, diagonal)
+        scalar_sums(2, PACK, diagonals[0])
+        multiply(1)
+        scalar_sums(2, PACK - 1, diagonals[1])
+        finish(1)
+        shared_sum(2, *steps[-1])
+        multiply(2)
+        finish(2)

from contextlib import ExitStack

import concourse.mybir as mybir

K, T, S, H, N, U = 1024, 2048, 512, 512, 128, 1024
FLOPS = 2 * K * H * S + 2 * H * N * U

F32 = mybir.dt.float32
BF16 = mybir.dt.bfloat16
I32 = mybir.dt.int32
U32 = mybir.dt.uint32
U16 = mybir.dt.uint16
U8 = mybir.dt.uint8
FP8X4 = mybir.dt.float8_e4m3fn_x4
COPY = mybir.ActivationFunctionType.Copy
ADD = mybir.AluOpType.add
MULT = mybir.AluOpType.mult

P = 128
PACK = 4
K_PASS = P * PACK
PASSES = K // K_PASS
QUADRANT = 32
SCALE_ROWS = 4
GROUP = 16
LINE = 4
BANKS = 8
SPARE = 32
CHUNKS = (512, 384, 128)
W1_ON_VECTOR = 76
HALVED_TILES = 3
CORNER_BUFFERS = 8


def tile_picked_yquadfm_mul_p_kernel(tc, x_words, x_scales, w1, unit, w2, offs, f1, f2, f3, f4, out):
    nc = tc.nc
    with ExitStack() as ctx:
        keep = ctx.enter_context(tc.tile_pool(name="keep", bufs=1))
        ring = ctx.enter_context(tc.tile_pool(name="ring", bufs=CORNER_BUFFERS))
        psum = ctx.enter_context(tc.psum_pool(name="psum", bufs=1))

        picks = keep.tile([P, S // GROUP], U16, name="picks")
        list1, list2, list3, list4 = [keep.tile([P, U // GROUP], U16, name=f"list{i}") for i in range(1, 5)]
        word_tables = [keep.tile([P, T], U32, name=f"word_table{o}") for o in range(PASSES)]
        scale_table = keep.tile([P, T], U8, name="scale_table")
        w1_raw = [keep.tile([P, PACK, H], F32, name=f"w1_raw{o}") for o in range(PASSES)]
        w2_raw = keep.tile([P, PACK, N], F32, name="w2_raw")
        unit_sb = keep.tile([P, PACK], F32, name="unit_sb")
        y_plain = [keep.tile([P, S + SPARE], F32, name=f"y_plain{t}") for t in range(PACK)]
        y_unit = [keep.tile([P, S + SPARE], F32, name=f"y_unit{t}") for t in range(PACK)]

        nc.vector.memset(scale_table[:].bitcast(I32), 0)
        for window in y_plain + y_unit:
            nc.vector.memset(window[:, S:], 0.0)

        def load_w1(o):
            rows = w1[o * K_PASS : (o + 1) * K_PASS, :]
            nc.sync.dma_start(out=w1_raw[o][:], in_=rows.rearrange("(p j) c -> p j c", j=PACK))

        def load_words(o):
            words = x_words[o].rearrange("p c r -> p (c r)")
            nc.sync.dma_start(out=word_tables[o][:].bitcast(I32), in_=words.bitcast(I32))

        load_w1(0)
        for q in range(P // QUADRANT):
            nc.sync.dma_start(
                out=scale_table[QUADRANT * q : QUADRANT * q + SCALE_ROWS * PASSES, :].bitcast(I32),
                in_=x_scales.bitcast(I32)[:, SCALE_ROWS * q : SCALE_ROWS * (q + 1), :],
            )
        nc.sync.dma_start(picks[:], offs)
        load_words(0)
        load_w1(1)
        load_words(1)
        nc.sync.dma_start(out=unit_sb[:], in_=unit.rearrange("(p t) o -> p (t o)", t=PACK))
        nc.sync.dma_start(out=w2_raw[:], in_=w2.rearrange("(p j) m -> p j m", j=PACK))
        for tile, face_list in ((list2, f2), (list4, f4), (list1, f1), (list3, f3)):
            nc.sync.dma_start(tile[:], face_list)

        def quantise(grouped, width, name):
            codes = keep.tile([P, width], U32, name=f"{name}_codes", align_bytes=64)
            scales = keep.tile([P, width], U8, name=f"{name}_scales", align_bytes=64)
            nc.vector.quantize_mx(out=codes[:].bitcast(FP8X4), scales=scales[:], in_=grouped)
            return codes, scales

        def quantise_w1(o):
            grouped = keep.tile([P, PACK, P, PACK], BF16, name=f"w1_grouped{o}", align_bytes=64)
            source = w1_raw[o][:].rearrange("p j (m t) -> p m j t", t=PACK)
            target = grouped[:].rearrange("p t m j -> p m j t")
            nc.vector.tensor_copy(target[:, :W1_ON_VECTOR], source[:, :W1_ON_VECTOR])
            nc.scalar.activation(target[:, W1_ON_VECTOR:], source[:, W1_ON_VECTOR:], COPY)
            return quantise(grouped[:].rearrange("p t m j -> p (t m j)"), H, f"w1_{o}")

        def entries(index_list, span):
            return index_list[:, span.start // GROUP : span.stop // GROUP]

        whole = slice(0, S)
        halves = (slice(0, S // 2), slice(S // 2, S))
        x_scale = keep.tile([P, S], U8, name="x_scale", align_bytes=64)
        x_codes = [keep.tile([P, S], U32, name=f"x_codes{o}", align_bytes=64) for o in range(PASSES)]
        w1_mx = [quantise_w1(0)]
        nc.vector.tensor_copy(x_scale[:], scale_table[:].indirect(picks[:]))
        nc.vector.tensor_copy(x_codes[0][:], word_tables[0][:].indirect(picks[:]))
        w1_mx.append(quantise_w1(1))
        for half in halves:
            nc.vector.tensor_copy(x_codes[1][:, half], word_tables[1][:].indirect(entries(picks, half)))

        pieces = [(t, half) for half in halves for t in range(HALVED_TILES)]
        pieces = pieces + [(t, whole) for t in range(HALVED_TILES, PACK)]
        y_banks = [psum.tile([P, span.stop - span.start], F32, name=f"bank{i}") for i, (t, span) in enumerate(pieces)]
        for o, (w1_codes, w1_scales) in enumerate(w1_mx):
            for bank, (t, span) in zip(y_banks, pieces):
                rows = slice(t * P, (t + 1) * P)
                nc.tensor.matmul_mx(
                    out=bank[:],
                    lhsT=w1_codes[:, rows].bitcast(FP8X4),
                    lhsT_scale=w1_scales[:, rows],
                    rhs=x_codes[o][:, span].bitcast(FP8X4),
                    rhs_scale=x_scale[SCALE_ROWS * o : P, span],
                    start=(o == 0),
                    stop=(o == PASSES - 1),
                )

        w2_grouped = keep.tile([P, N, PACK], BF16, name="w2_grouped", align_bytes=64)
        nc.scalar.activation(
            w2_grouped[:].rearrange("p (c i) j -> p c j i", i=LINE),
            w2_raw[:].rearrange("p j (c i) -> p c j i", i=LINE),
            COPY,
        )
        w2_codes, w2_scales = quantise(w2_grouped[:].rearrange("p m j -> p (m j)"), N, "w2")

        for bank, (t, span) in zip(y_banks, pieces):
            if t == 0:
                nc.scalar.activation(y_plain[t][:, span], bank[:], COPY)
            else:
                nc.vector.tensor_copy(y_plain[t][:, span], bank[:])
        for t in range(PACK):
            nc.vector.tensor_scalar(y_unit[t][:, :S], y_plain[t][:, :S], unit_sb[:, t : t + 1], None, MULT)

        starts = [sum(CHUNKS[:c]) for c in range(len(CHUNKS))]
        faces = [slice(start, start + n) for start, n in zip(starts, CHUNKS)]
        dia = [keep.tile([P, PACK, n], F32, name=f"dia{c}") for c, n in enumerate(CHUNKS)]
        dib = [keep.tile([P, PACK, n], F32, name=f"dib{c}") for c, n in enumerate(CHUNKS)]
        hid = [keep.tile([P, n, PACK], BF16, name=f"hid{c}", align_bytes=64) for c, n in enumerate(CHUNKS)]
        diagonals = ((dib, y_plain, list2, list4), (dia, y_unit, list1, list3))

        def gather_on_scalar(target, window, index_list, c):
            nc.scalar.activation(target, window[:].indirect(entries(index_list, faces[c])), COPY)

        def shared_sum(c, t, diagonal):
            sums, windows, first, second = diagonal
            corner = ring.tile([P, CHUNKS[c]], F32, name="corner")
            gather_on_scalar(corner[:], windows[t], first, c)
            nc.vector.tensor_tensor(sums[c][:, t, :], windows[t][:].indirect(entries(second, faces[c])), corner[:], ADD)

        def scalar_sums(c, tiles, diagonal):
            sums, windows, first, second = diagonal
            pair = [ring.tile([P, tiles, CHUNKS[c]], F32, name="corner") for index_list in (first, second)]
            for t in range(tiles):
                for corner, index_list in zip(pair, (first, second)):
                    gather_on_scalar(corner[:, t, :], windows[t], index_list, c)
            nc.vector.tensor_tensor(sums[c][:, :tiles, :], pair[0][:], pair[1][:], ADD)

        def multiply(c):
            nc.vector.tensor_tensor(
                hid[c][:].rearrange("p (g i) t -> p g t i", i=LINE),
                dia[c][:].rearrange("p t (g i) -> p g t i", i=LINE),
                dib[c][:].rearrange("p t (g i) -> p g t i", i=LINE),
                MULT,
            )

        def finish(c):
            n = CHUNKS[c]
            hid_codes, hid_scales = quantise(hid[c][:].rearrange("p r t -> p (r t)"), n, f"hid{c}")
            acc = psum.tile([P, n], F32, name=f"bank{(len(pieces) + c) % BANKS}")
            done = 0
            for width in (512, 256, 128):
                if n - done >= width:
                    span = slice(done, done + width)
                    nc.tensor.matmul_mx(
                        out=acc[:, span],
                        lhsT=w2_codes[:].bitcast(FP8X4),
                        lhsT_scale=w2_scales[:],
                        rhs=hid_codes[:, span].bitcast(FP8X4),
                        rhs_scale=hid_scales[:, span],
                        start=True,
                        stop=True,
                    )
                    done = done + width
            result = keep.tile([P, n], F32, name=f"result{c}")
            nc.scalar.activation(result[:], acc[:], COPY)
            nc.sync.dma_start(out=out[:, faces[c]], in_=result[:])

        steps = [(t, diagonal) for t in range(PACK) for diagonal in diagonals]
        for t, diagonal in steps:
            shared_sum(0, t, diagonal)
        shared_sum(1, *steps[0])
        multiply(0)
        shared_sum(1, *steps[1])
        finish(0)
        for t, diagonal in steps[2:]:
            shared_sum(1, t, diagonal)
        scalar_sums(2, PACK, diagonals[0])
        multiply(1)
        scalar_sums(2, PACK - 1, diagonals[1])
        finish(1)
        shared_sum(2, *steps[-1])
        multiply(2)
        finish(2)
